import numpy as np
import ml_dtypes


def mxq(x, axis, fmt="e4m3"):
    dtype, down = {"e4m3": (ml_dtypes.float8_e4m3fn, 7), "e5m2": (ml_dtypes.float8_e5m2, 14)}[fmt]
    v = np.moveaxis(np.asarray(x, np.float32).astype(ml_dtypes.bfloat16).astype(np.float64), axis, -1)
    blocks = v.reshape(v.shape[:-1] + (-1, 32))
    amax = np.abs(blocks).max(-1, keepdims=True)
    byte = np.maximum(np.where(amax > 0, np.frexp(amax)[1] - 1 + 127, 0) - down, 1)
    scale = np.exp2(byte - 127.0)
    codes = (blocks / scale).astype(np.float32).astype(dtype).astype(np.float64)
    return np.moveaxis((codes * scale).reshape(v.shape), -1, axis)


WIDE = False


def mx_kscale(k):
    if not WIDE:
        return np.ones(k)
    levels = np.array([10, -10, 5, -5, 0])
    if k % 512:
        return np.exp2(np.random.permutation(np.resize(levels, k // 32))).repeat(32)
    a = np.empty((k // 512, 16))
    for p in range(k // 512):
        a[p, :8] = np.random.permutation(np.resize(levels, 8))
        for g in range(8):
            far = levels[np.abs(levels - a[p, g]) >= 10]
            a[p, g + 8] = far[np.random.randint(len(far))]
    return np.exp2(a.ravel()).repeat(32)


def f64(x):
    return np.asarray(x).astype(np.float64)


def striped(idx):
    return np.tile(np.asarray(idx).reshape(-1, 16).T, (8, 1)).astype(np.uint16)


def unstriped(offs):
    return offs[:16].T.reshape(-1).astype(np.int64)


def striped8(idx):
    return np.asarray(idx).reshape(8, -1, 16).transpose(0, 2, 1).reshape(128, -1).astype(np.uint16)


def unstriped8(offs):
    return offs.reshape(8, 16, -1).transpose(0, 2, 1).reshape(8, -1).astype(np.int64)


def pick8(x, idx, run):
    r = np.arange(len(x))
    return x[r[:, None], idx[r % (8 * run) // run]]


E2M1 = np.array([0.0, 0.5, 1.0, 1.5, 2.0, 3.0, 4.0, 6.0, -0.0, -0.5, -1.0, -1.5, -2.0, -3.0, -4.0, -6.0])


def pack_weight(w, fmt):
    k, n = w.shape
    w = f64(np.asarray(w, np.float32).astype(ml_dtypes.bfloat16)).reshape(k // 32, 32, n)
    amax = np.abs(w).max(1)
    if fmt == "e4m3":
        byte = np.frexp(amax)[1] - 1 + 127 - 7
    else:
        mant, ex = np.frexp(amax / 6.0)
        byte = np.where(mant > 0.5, ex, ex - 1) + 127
    byte = np.clip(np.where(amax > 0, byte, 1), 1, 254)
    scaled = (w * np.exp2(127.0 - byte)[:, None, :]).reshape(k, n).astype(np.float32)
    by_word = np.ascontiguousarray(scaled.reshape(k // 512, 128, 4, n).transpose(0, 1, 3, 2))
    if fmt == "e4m3":
        words = by_word.astype(ml_dtypes.float8_e4m3fn).view(np.uint8)
    else:
        c = by_word.astype(ml_dtypes.float4_e2m1fn).view(np.uint8) & 0xF
        words = (c[..., 0::2] | (c[..., 1::2] << 4)).reshape(k // 512, 128, 2 * n)
    return np.ascontiguousarray(words), np.ascontiguousarray(byte.astype(np.uint8).reshape(k // 512, 16, n))


def unpack_weight(words, scales, fmt):
    g, _, n = scales.shape
    words = np.ascontiguousarray(words).reshape(g, 128, n, -1)
    if fmt == "e4m3":
        vals = words.view(ml_dtypes.float8_e4m3fn).astype(np.float64)
    else:
        nib = np.empty((g, 128, n, 4), np.uint8)
        nib[..., 0::2] = words & 0xF
        nib[..., 1::2] = words >> 4
        vals = E2M1[nib]
    vals = vals * np.repeat(np.exp2(scales.astype(np.float64) - 127.0), 8, axis=1)[..., None]
    return vals.transpose(0, 1, 3, 2).reshape(g * 512, n)


K, T, J, L, V, N = 1024, 2048, 512, 512, 512, 512


def setup_inputs():
    n = np.random.standard_normal
    idx = np.random.permutation(T)[:J]
    idx2 = np.stack([np.random.randint(0, V, J) for _ in range(8)])
    fk = mx_kscale(K)
    fl = mx_kscale(L)
    xtp = pack_weight(n((K, T)) / fk[:, None], "e4m3")
    cdp = pack_weight(n((L, V)) / fl[:, None], "e2m1")
    wcp = pack_weight(n((L, N)) * 1 / np.sqrt(L) * fl[:, None], "e4m3")
    return {
        "xt_words": xtp[0],
        "xt_scales": xtp[1],
        "w": (n((K, N)) * 1 / np.sqrt(K) * fk[:, None]).astype(np.float32),
        "cd_words": cdp[0],
        "cd_scales": cdp[1],
        "wc_words": wcp[0],
        "wc_scales": wcp[1],
        "offs": striped(idx),
        "offs2": striped8(idx2),
    }


def reference(xt_words, xt_scales, w, cd_words, cd_scales, wc_words, wc_scales, offs, offs2):
    idx = unstriped(offs)
    idx2 = unstriped8(offs2)
    xtu = unpack_weight(xt_words, xt_scales, "e4m3")
    cdu = unpack_weight(cd_words, cd_scales, "e2m1")
    wcu = unpack_weight(wc_words, wc_scales, "e4m3")
    wq = mxq(f64(w), 0, "e4m3")
    xtidxg = xtu[:, idx]
    p = wq.T @ xtidxg
    e = wcu.T @ cdu
    y = np.maximum(p + pick8(e, idx2, 64), 0.0)
    return y

@@ -1,0 +1,154 @@
+from contextlib import ExitStack
+
+import concourse.mybir as mybir
+
+K, T, J, L, V, N = 1024, 2048, 512, 512, 512, 512
+FLOPS = 2 * (K * N * J + L * N * V)
+
+F32 = mybir.dt.float32
+BF16 = mybir.dt.bfloat16
+I32 = mybir.dt.int32
+U32 = mybir.dt.uint32
+U16 = mybir.dt.uint16
+U8 = mybir.dt.uint8
+FP8X4 = mybir.dt.float8_e4m3fn_x4
+FP4X4 = mybir.dt.float4_e2m1fn_x4
+ACT = mybir.ActivationFunctionType
+ALU = mybir.AluOpType
+
+P = 128
+PACK = 4
+K_PASS = P * PACK
+PASSES = K // K_PASS
+TILES = N // P
+HALVES = 2
+HALF = J // HALVES
+LIST_COLS = J // 16
+
+
+def tile_list_head_tables_kernel(tc, xt_words, xt_scales, w, cd_words, cd_scales, wc_words, wc_scales, offs, offs2, out):
+    nc = tc.nc
+    with ExitStack() as ctx:
+        keep = ctx.enter_context(tc.tile_pool(name="keep", bufs=1))
+        psum = ctx.enter_context(tc.psum_pool(name="psum", bufs=8))
+
+        tok_list = keep.tile([P, LIST_COLS], U16, name="tok_list")
+        head_lists = keep.tile([P, LIST_COLS], U16, name="head_lists")
+        wc_raw = keep.tile([P, N], I32, name="wc_raw", align_bytes=64)
+        cd_codes = keep.tile([P, 2 * V], U8, name="cd_codes", align_bytes=64)
+        small_scales = keep.tile([P, N + V], U8, name="small_scales", align_bytes=64)
+        xt_scale_rows = keep.tile([P, T], U8, name="xt_scale_rows", align_bytes=64)
+        xt_table = [keep.tile([P, T], I32, name="xt_table%d" % z, align_bytes=64) for z in range(PASSES)]
+        w_raw = [keep.tile([P, PACK, N], F32, name="w_raw%d" % z, align_bytes=64) for z in range(PASSES)]
+
+        nc.vector.memset(small_scales[:].bitcast(I32), 0)
+        nc.vector.memset(xt_scale_rows[:].bitcast(I32), 0)
+
+        def load_w(z):
+            nc.sync.dma_start(out=w_raw[z][:], in_=w[z * K_PASS : (z + 1) * K_PASS, :].rearrange("(p j) n -> p j n", j=PACK))
+
+        def load_xt(z):
+            nc.sync.dma_start(out=xt_table[z][:], in_=xt_words[z].rearrange("p c r -> p (c r)").bitcast(I32))
+
+        for q in range(4):
+            nc.gpsimd.dma_start(out=small_scales[32 * q : 32 * q + 4, N : N + V].bitcast(I32), in_=cd_scales[0, 4 * q : 4 * q + 4, :].bitcast(I32))
+        nc.sync.dma_start(out=wc_raw[:], in_=wc_words[0].rearrange("p c r -> p (c r)").bitcast(I32))
+        nc.sync.dma_start(out=cd_codes[:].bitcast(I32), in_=cd_words[0].bitcast(I32))
+        for q in range(4):
+            nc.sync.dma_start(out=small_scales[32 * q : 32 * q + 4, 0:N].bitcast(I32), in_=wc_scales[0, 4 * q : 4 * q + 4, :].bitcast(I32))
+        load_w(0)
+        nc.sync.dma_start(head_lists[:], offs2)
+        load_xt(0)
+        for q in range(4):
+            nc.sync.dma_start(out=xt_scale_rows[32 * q : 32 * q + 8, :].bitcast(I32), in_=xt_scales[:, 4 * q : 4 * q + 4, :].bitcast(I32))
+        nc.sync.dma_start(tok_list[:], offs)
+        load_w(1)
+        load_xt(1)
+
+        wc_codes = keep.tile([P, N], U32, name="wc_codes", align_bytes=64)
+        wc_plane = keep.tile([P, N], U8, name="wc_plane", align_bytes=64)
+        nc.vector.tensor_copy(
+            out=wc_codes[:].rearrange("p (t m) -> p m t", t=TILES),
+            in_=wc_raw[:].bitcast(U32).rearrange("p (m t) -> p m t", t=TILES),
+        )
+        nc.vector.tensor_copy(
+            out=wc_plane[:].rearrange("p (t m) -> p m t", t=TILES),
+            in_=small_scales[:, 0:N].rearrange("p (m t) -> p m t", t=TILES),
+        )
+
+        picked = []
+        for t in range(TILES):
+            cols = slice(t * P, (t + 1) * P)
+            e_bank = psum.tile([P, V], F32, name="bank", tag="bank")
+            nc.tensor.matmul_mx(
+                out=e_bank[:],
+                lhsT=wc_codes[:, cols].bitcast(FP8X4),
+                lhsT_scale=wc_plane[:, cols],
+                rhs=cd_codes[:].bitcast(FP4X4),
+                rhs_scale=small_scales[:, N : N + V],
+                start=True,
+                stop=True,
+            )
+            e_rows = keep.tile([P, V], F32, name="e_rows%d" % t)
+            nc.scalar.copy(out=e_rows[:], in_=e_bank[:])
+            picked.append((e_rows, keep.tile([P, J], F32, name="picked%d" % t)))
+
+        def list_half(lists, h):
+            return lists[:, h * LIST_COLS // HALVES : (h + 1) * LIST_COLS // HALVES]
+
+        for h in range(HALVES):
+            for t in range(TILES):
+                e_rows, dst = picked[t]
+                nc.scalar.activation(out=dst[:, h * HALF : (h + 1) * HALF], in_=e_rows[:].indirect(list_half(head_lists, h)), func=ACT.Copy)
+
+        w_codes = [keep.tile([P, N], U32, name="w_codes%d" % z, align_bytes=64) for z in range(PASSES)]
+        w_plane = [keep.tile([P, N], U8, name="w_plane%d" % z, align_bytes=64) for z in range(PASSES)]
+        x_codes = [keep.tile([P, J], U32, name="x_codes%d" % z, align_bytes=64) for z in range(PASSES)]
+        x_planes = keep.tile([P, J], U8, name="x_planes", align_bytes=64)
+
+        def quantise_w(z):
+            grouped = keep.tile([P, N * PACK], BF16, name="w_grouped%d" % z, align_bytes=64)
+            nc.vector.tensor_copy(
+                out=grouped[:].rearrange("p (t m j) -> p m j t", t=TILES, j=PACK),
+                in_=w_raw[z][:].rearrange("p j (m t) -> p m j t", t=TILES),
+            )
+            nc.vector.quantize_mx(out=w_codes[z][:].bitcast(FP8X4), scales=w_plane[z][:], in_=grouped[:])
+
+        quantise_w(0)
+        nc.vector.tensor_copy(out=x_codes[0][:], in_=xt_table[0][:].bitcast(U32).indirect(tok_list[:]))
+        nc.vector.tensor_copy(out=x_planes[:], in_=xt_scale_rows[:].indirect(tok_list[:]))
+        quantise_w(1)
+        for h in range(HALVES):
+            nc.vector.tensor_copy(
+                out=x_codes[1][:, h * HALF : (h + 1) * HALF],
+                in_=xt_table[1][:].bitcast(U32).indirect(list_half(tok_list, h)),
+            )
+
+        units = [(h, t) for h in range(HALVES) for t in range(TILES)]
+        banks = {}
+
+        def p_pass(z, h, t):
+            cols = slice(t * P, (t + 1) * P)
+            slots = slice(h * HALF, (h + 1) * HALF)
+            nc.tensor.matmul_mx(
+                out=banks[h, t][:],
+                lhsT=w_codes[z][:, cols].bitcast(FP8X4),
+                lhsT_scale=w_plane[z][:, cols],
+                rhs=x_codes[z][:, slots].bitcast(FP8X4),
+                rhs_scale=x_planes[4 * z :, slots],
+                start=(z == 0),
+                stop=(z == PASSES - 1),
+            )
+
+        for h, t in units:
+            banks[h, t] = psum.tile([P, HALF], F32, name="bank", tag="bank")
+            p_pass(0, h, t)
+        out_rows = out.rearrange("(p t) j -> p t j", t=TILES)
+        for h, t in units:
+            slots = slice(h * HALF, (h + 1) * HALF)
+            p_pass(1, h, t)
+            total = keep.tile([P, HALF], F32, name="total%d%d" % (h, t))
+            result = keep.tile([P, HALF], F32, name="result%d%d" % (h, t))
+            nc.vector.tensor_tensor(out=total[:], in0=banks[h, t][:], in1=picked[t][1][:, slots], op=ALU.add)
+            nc.scalar.activation(out=result[:], in_=total[:], func=ACT.Relu)
+            nc.sync.dma_start(out=out_rows[:, t, slots], in_=result[:])

@@ -36,33 +36,39 @@ def tile_list_head_tables_kernel(tc, xt_words, xt_scales, w, cd_words, cd_scales
         head_lists = keep.tile([P, LIST_COLS], U16, name="head_lists")
         wc_raw = keep.tile([P, N], I32, name="wc_raw", align_bytes=64)
         cd_codes = keep.tile([P, 2 * V], U8, name="cd_codes", align_bytes=64)
-        small_scales = keep.tile([P, N + V], U8, name="small_scales", align_bytes=64)
+        wc_rows = keep.tile([P, N // 4], I32, name="wc_rows")
+        cd_plane = keep.tile([P, V], U8, name="cd_plane", align_bytes=64)
+        small_scales = keep.tile([P, N], U8, name="small_scales", align_bytes=64)
         xt_scale_rows = keep.tile([P, T], U8, name="xt_scale_rows", align_bytes=64)
         xt_table = [keep.tile([P, T], I32, name="xt_table%d" % z, align_bytes=64) for z in range(PASSES)]
-        w_raw = [keep.tile([P, PACK, N], F32, name="w_raw%d" % z, align_bytes=64) for z in range(PASSES)]
+        w_raw = [[keep.tile([P, 2, N], F32, name="w_raw%d%d" % (z, u), align_bytes=64) for u in range(2)] for z in range(PASSES)]
 
-        nc.vector.memset(small_scales[:].bitcast(I32), 0)
+        nc.vector.memset(cd_plane[:].bitcast(I32), 0)
         nc.vector.memset(xt_scale_rows[:].bitcast(I32), 0)
+        nc.vector.memset(small_scales[:].bitcast(I32), 0)
 
-        def load_w(z):
-            nc.sync.dma_start(out=w_raw[z][:], in_=w[z * K_PASS : (z + 1) * K_PASS, :].rearrange("(p j) n -> p j n", j=PACK))
+        def load_w(z, u):
+            rows = w[z * K_PASS : (z + 1) * K_PASS, :].rearrange("(p j) n -> p j n", j=PACK)
+            nc.sync.dma_start(out=w_raw[z][u][:], in_=rows[:, 2 * u : 2 * u + 2, :])
 
         def load_xt(z):
             nc.sync.dma_start(out=xt_table[z][:], in_=xt_words[z].rearrange("p c r -> p (c r)").bitcast(I32))
 
-        for q in range(4):
-            nc.gpsimd.dma_start(out=small_scales[32 * q : 32 * q + 4, N : N + V].bitcast(I32), in_=cd_scales[0, 4 * q : 4 * q + 4, :].bitcast(I32))
         nc.sync.dma_start(out=wc_raw[:], in_=wc_words[0].rearrange("p c r -> p (c r)").bitcast(I32))
         nc.sync.dma_start(out=cd_codes[:].bitcast(I32), in_=cd_words[0].bitcast(I32))
         for q in range(4):
-            nc.sync.dma_start(out=small_scales[32 * q : 32 * q + 4, 0:N].bitcast(I32), in_=wc_scales[0, 4 * q : 4 * q + 4, :].bitcast(I32))
-        load_w(0)
+            nc.sync.dma_start(out=wc_rows[32 * q : 32 * q + 4, :], in_=wc_scales[0, 4 * q : 4 * q + 4, :].bitcast(I32))
+        load_w(0, 0)
+        load_w(0, 1)
+        for q in range(4):
+            nc.sync.dma_start(out=cd_plane[32 * q : 32 * q + 4, :].bitcast(I32), in_=cd_scales[0, 4 * q : 4 * q + 4, :].bitcast(I32))
         nc.sync.dma_start(head_lists[:], offs2)
-        load_xt(0)
+        load_w(1, 0)
+        load_w(1, 1)
+        nc.sync.dma_start(tok_list[:], offs)
         for q in range(4):
             nc.sync.dma_start(out=xt_scale_rows[32 * q : 32 * q + 8, :].bitcast(I32), in_=xt_scales[:, 4 * q : 4 * q + 4, :].bitcast(I32))
-        nc.sync.dma_start(tok_list[:], offs)
-        load_w(1)
+        load_xt(0)
         load_xt(1)
 
         wc_codes = keep.tile([P, N], U32, name="wc_codes", align_bytes=64)
@@ -71,10 +77,32 @@ def tile_list_head_tables_kernel(tc, xt_words, xt_scales, w, cd_words, cd_scales
             out=wc_codes[:].rearrange("p (t m) -> p m t", t=TILES),
             in_=wc_raw[:].bitcast(U32).rearrange("p (m t) -> p m t", t=TILES),
         )
+        for q in range(4):
+            nc.vector.tensor_copy(out=small_scales[32 * q : 32 * q + 4, 0:N].bitcast(I32), in_=wc_rows[32 * q : 32 * q + 4, :])
         nc.vector.tensor_copy(
             out=wc_plane[:].rearrange("p (t m) -> p m t", t=TILES),
             in_=small_scales[:, 0:N].rearrange("p (m t) -> p m t", t=TILES),
         )
+
+        w_codes = [keep.tile([P, N], U32, name="w_codes%d" % z, align_bytes=64) for z in range(PASSES)]
+        w_plane = [keep.tile([P, N], U8, name="w_plane%d" % z, align_bytes=64) for z in range(PASSES)]
+        x_codes = [keep.tile([P, J], U32, name="x_codes%d" % z, align_bytes=64) for z in range(PASSES)]
+        x_planes = keep.tile([P, J], U8, name="x_planes", align_bytes=64)
+
+        w_grouped = [keep.tile([P, N * PACK], BF16, name="w_grouped%d" % z, align_bytes=64) for z in range(PASSES)]
+
+        def round_w(z, u, copy):
+            copy(
+                out=w_grouped[z][:].rearrange("p (t m j) -> p m j t", t=TILES, j=PACK)[:, :, 2 * u : 2 * u + 2, :],
+                in_=w_raw[z][u][:].rearrange("p j (m t) -> p m j t", t=TILES),
+            )
+
+        def quantise_w(z):
+            nc.vector.quantize_mx(out=w_codes[z][:].bitcast(FP8X4), scales=w_plane[z][:], in_=w_grouped[z][:])
+
+        round_w(0, 0, nc.scalar.copy)
+        round_w(0, 1, nc.vector.tensor_copy)
+        quantise_w(0)
 
         picked = []
         for t in range(TILES):
@@ -85,7 +113,7 @@ def tile_list_head_tables_kernel(tc, xt_words, xt_scales, w, cd_words, cd_scales
                 lhsT=wc_codes[:, cols].bitcast(FP8X4),
                 lhsT_scale=wc_plane[:, cols],
                 rhs=cd_codes[:].bitcast(FP4X4),
-                rhs_scale=small_scales[:, N : N + V],
+                rhs_scale=cd_plane[:],
                 start=True,
                 stop=True,
             )
@@ -101,28 +129,17 @@ def tile_list_head_tables_kernel(tc, xt_words, xt_scales, w, cd_words, cd_scales
                 e_rows, dst = picked[t]
                 nc.scalar.activation(out=dst[:, h * HALF : (h + 1) * HALF], in_=e_rows[:].indirect(list_half(head_lists, h)), func=ACT.Copy)
 
-        w_codes = [keep.tile([P, N], U32, name="w_codes%d" % z, align_bytes=64) for z in range(PASSES)]
-        w_plane = [keep.tile([P, N], U8, name="w_plane%d" % z, align_bytes=64) for z in range(PASSES)]
-        x_codes = [keep.tile([P, J], U32, name="x_codes%d" % z, align_bytes=64) for z in range(PASSES)]
-        x_planes = keep.tile([P, J], U8, name="x_planes", align_bytes=64)
-
-        def quantise_w(z):
-            grouped = keep.tile([P, N * PACK], BF16, name="w_grouped%d" % z, align_bytes=64)
-            nc.vector.tensor_copy(
-                out=grouped[:].rearrange("p (t m j) -> p m j t", t=TILES, j=PACK),
-                in_=w_raw[z][:].rearrange("p j (m t) -> p m j t", t=TILES),
-            )
-            nc.vector.quantize_mx(out=w_codes[z][:].bitcast(FP8X4), scales=w_plane[z][:], in_=grouped[:])
-
-        quantise_w(0)
-        nc.vector.tensor_copy(out=x_codes[0][:], in_=xt_table[0][:].bitcast(U32).indirect(tok_list[:]))
-        nc.vector.tensor_copy(out=x_planes[:], in_=xt_scale_rows[:].indirect(tok_list[:]))
+        round_w(1, 0, nc.vector.tensor_copy)
+        round_w(1, 1, nc.vector.tensor_copy)
         quantise_w(1)
-        for h in range(HALVES):
-            nc.vector.tensor_copy(
-                out=x_codes[1][:, h * HALF : (h + 1) * HALF],
-                in_=xt_table[1][:].bitcast(U32).indirect(list_half(tok_list, h)),
-            )
+        for z in range(PASSES):
+            for h in range(HALVES):
+                if z == 0:
+                    nc.vector.tensor_copy(out=x_planes[:, h * HALF : (h + 1) * HALF], in_=xt_scale_rows[:].indirect(list_half(tok_list, h)))
+                nc.vector.tensor_copy(
+                    out=x_codes[z][:, h * HALF : (h + 1) * HALF],
+                    in_=xt_table[z][:].bitcast(U32).indirect(list_half(tok_list, h)),
+                )
 
         units = [(h, t) for h in range(HALVES) for t in range(TILES)]
         banks = {}

from contextlib import ExitStack

import concourse.mybir as mybir

K, T, J, L, V, N = 1024, 2048, 512, 512, 512, 512
FLOPS = 2 * (K * N * J + L * N * V)

F32 = mybir.dt.float32
BF16 = mybir.dt.bfloat16
I32 = mybir.dt.int32
U32 = mybir.dt.uint32
U16 = mybir.dt.uint16
U8 = mybir.dt.uint8
FP8X4 = mybir.dt.float8_e4m3fn_x4
FP4X4 = mybir.dt.float4_e2m1fn_x4
ACT = mybir.ActivationFunctionType
ALU = mybir.AluOpType

P = 128
PACK = 4
K_PASS = P * PACK
PASSES = K // K_PASS
TILES = N // P
HALVES = 2
HALF = J // HALVES
LIST_COLS = J // 16


def tile_list_head_tables_kernel(tc, xt_words, xt_scales, w, cd_words, cd_scales, wc_words, wc_scales, offs, offs2, out):
    nc = tc.nc
    with ExitStack() as ctx:
        keep = ctx.enter_context(tc.tile_pool(name="keep", bufs=1))
        psum = ctx.enter_context(tc.psum_pool(name="psum", bufs=8))

        tok_list = keep.tile([P, LIST_COLS], U16, name="tok_list")
        head_lists = keep.tile([P, LIST_COLS], U16, name="head_lists")
        wc_raw = keep.tile([P, N], I32, name="wc_raw", align_bytes=64)
        cd_codes = keep.tile([P, 2 * V], U8, name="cd_codes", align_bytes=64)
        wc_rows = keep.tile([P, N // 4], I32, name="wc_rows")
        cd_plane = keep.tile([P, V], U8, name="cd_plane", align_bytes=64)
        small_scales = keep.tile([P, N], U8, name="small_scales", align_bytes=64)
        xt_scale_rows = keep.tile([P, T], U8, name="xt_scale_rows", align_bytes=64)
        xt_table = [keep.tile([P, T], I32, name="xt_table%d" % z, align_bytes=64) for z in range(PASSES)]
        w_raw = [[keep.tile([P, 2, N], F32, name="w_raw%d%d" % (z, u), align_bytes=64) for u in range(2)] for z in range(PASSES)]

        nc.vector.memset(cd_plane[:].bitcast(I32), 0)
        nc.vector.memset(xt_scale_rows[:].bitcast(I32), 0)
        nc.vector.memset(small_scales[:].bitcast(I32), 0)

        def load_w(z, u):
            rows = w[z * K_PASS : (z + 1) * K_PASS, :].rearrange("(p j) n -> p j n", j=PACK)
            nc.sync.dma_start(out=w_raw[z][u][:], in_=rows[:, 2 * u : 2 * u + 2, :])

        def load_xt(z):
            nc.sync.dma_start(out=xt_table[z][:], in_=xt_words[z].rearrange("p c r -> p (c r)").bitcast(I32))

        nc.sync.dma_start(out=wc_raw[:], in_=wc_words[0].rearrange("p c r -> p (c r)").bitcast(I32))
        nc.sync.dma_start(out=cd_codes[:].bitcast(I32), in_=cd_words[0].bitcast(I32))
        for q in range(4):
            nc.sync.dma_start(out=wc_rows[32 * q : 32 * q + 4, :], in_=wc_scales[0, 4 * q : 4 * q + 4, :].bitcast(I32))
        load_w(0, 0)
        load_w(0, 1)
        for q in range(4):
            nc.sync.dma_start(out=cd_plane[32 * q : 32 * q + 4, :].bitcast(I32), in_=cd_scales[0, 4 * q : 4 * q + 4, :].bitcast(I32))
        nc.sync.dma_start(head_lists[:], offs2)
        load_w(1, 0)
        load_w(1, 1)
        nc.sync.dma_start(tok_list[:], offs)
        for q in range(4):
            nc.sync.dma_start(out=xt_scale_rows[32 * q : 32 * q + 8, :].bitcast(I32), in_=xt_scales[:, 4 * q : 4 * q + 4, :].bitcast(I32))
        load_xt(0)
        load_xt(1)

        wc_codes = keep.tile([P, N], U32, name="wc_codes", align_bytes=64)
        wc_plane = keep.tile([P, N], U8, name="wc_plane", align_bytes=64)
        nc.vector.tensor_copy(
            out=wc_codes[:].rearrange("p (t m) -> p m t", t=TILES),
            in_=wc_raw[:].bitcast(U32).rearrange("p (m t) -> p m t", t=TILES),
        )
        for q in range(4):
            nc.vector.tensor_copy(out=small_scales[32 * q : 32 * q + 4, 0:N].bitcast(I32), in_=wc_rows[32 * q : 32 * q + 4, :])
        nc.vector.tensor_copy(
            out=wc_plane[:].rearrange("p (t m) -> p m t", t=TILES),
            in_=small_scales[:, 0:N].rearrange("p (m t) -> p m t", t=TILES),
        )

        w_codes = [keep.tile([P, N], U32, name="w_codes%d" % z, align_bytes=64) for z in range(PASSES)]
        w_plane = [keep.tile([P, N], U8, name="w_plane%d" % z, align_bytes=64) for z in range(PASSES)]
        x_codes = [keep.tile([P, J], U32, name="x_codes%d" % z, align_bytes=64) for z in range(PASSES)]
        x_planes = keep.tile([P, J], U8, name="x_planes", align_bytes=64)

        w_grouped = [keep.tile([P, N * PACK], BF16, name="w_grouped%d" % z, align_bytes=64) for z in range(PASSES)]

        def round_w(z, u, copy):
            copy(
                out=w_grouped[z][:].rearrange("p (t m j) -> p m j t", t=TILES, j=PACK)[:, :, 2 * u : 2 * u + 2, :],
                in_=w_raw[z][u][:].rearrange("p j (m t) -> p m j t", t=TILES),
            )

        def quantise_w(z):
            nc.vector.quantize_mx(out=w_codes[z][:].bitcast(FP8X4), scales=w_plane[z][:], in_=w_grouped[z][:])

        round_w(0, 0, nc.scalar.copy)
        round_w(0, 1, nc.vector.tensor_copy)
        quantise_w(0)

        picked = []
        for t in range(TILES):
            cols = slice(t * P, (t + 1) * P)
            e_bank = psum.tile([P, V], F32, name="bank", tag="bank")
            nc.tensor.matmul_mx(
                out=e_bank[:],
                lhsT=wc_codes[:, cols].bitcast(FP8X4),
                lhsT_scale=wc_plane[:, cols],
                rhs=cd_codes[:].bitcast(FP4X4),
                rhs_scale=cd_plane[:],
                start=True,
                stop=True,
            )
            e_rows = keep.tile([P, V], F32, name="e_rows%d" % t)
            nc.scalar.copy(out=e_rows[:], in_=e_bank[:])
            picked.append((e_rows, keep.tile([P, J], F32, name="picked%d" % t)))

        def list_half(lists, h):
            return lists[:, h * LIST_COLS // HALVES : (h + 1) * LIST_COLS // HALVES]

        for h in range(HALVES):
            for t in range(TILES):
                e_rows, dst = picked[t]
                nc.scalar.activation(out=dst[:, h * HALF : (h + 1) * HALF], in_=e_rows[:].indirect(list_half(head_lists, h)), func=ACT.Copy)

        round_w(1, 0, nc.vector.tensor_copy)
        round_w(1, 1, nc.vector.tensor_copy)
        quantise_w(1)
        for z in range(PASSES):
            for h in range(HALVES):
                if z == 0:
                    nc.vector.tensor_copy(out=x_planes[:, h * HALF : (h + 1) * HALF], in_=xt_scale_rows[:].indirect(list_half(tok_list, h)))
                nc.vector.tensor_copy(
                    out=x_codes[z][:, h * HALF : (h + 1) * HALF],
                    in_=xt_table[z][:].bitcast(U32).indirect(list_half(tok_list, h)),
                )

        units = [(h, t) for h in range(HALVES) for t in range(TILES)]
        banks = {}

        def p_pass(z, h, t):
            cols = slice(t * P, (t + 1) * P)
            slots = slice(h * HALF, (h + 1) * HALF)
            nc.tensor.matmul_mx(
                out=banks[h, t][:],
                lhsT=w_codes[z][:, cols].bitcast(FP8X4),
                lhsT_scale=w_plane[z][:, cols],
                rhs=x_codes[z][:, slots].bitcast(FP8X4),
                rhs_scale=x_planes[4 * z :, slots],
                start=(z == 0),
                stop=(z == PASSES - 1),
            )

        for h, t in units:
            banks[h, t] = psum.tile([P, HALF], F32, name="bank", tag="bank")
            p_pass(0, h, t)
        out_rows = out.rearrange("(p t) j -> p t j", t=TILES)
        for h, t in units:
            slots = slice(h * HALF, (h + 1) * HALF)
            p_pass(1, h, t)
            total = keep.tile([P, HALF], F32, name="total%d%d" % (h, t))
            result = keep.tile([P, HALF], F32, name="result%d%d" % (h, t))
            nc.vector.tensor_tensor(out=total[:], in0=banks[h, t][:], in1=picked[t][1][:, slots], op=ALU.add)
            nc.scalar.activation(out=result[:], in_=total[:], func=ACT.Relu)
            nc.sync.dma_start(out=out_rows[:, t, slots], in_=result[:])
